import numpy as np
import ml_dtypes


def mxq(x, axis, fmt="e4m3"):
    dtype, down = {"e4m3": (ml_dtypes.float8_e4m3fn, 7), "e5m2": (ml_dtypes.float8_e5m2, 14)}[fmt]
    v = np.moveaxis(np.asarray(x, np.float32).astype(ml_dtypes.bfloat16).astype(np.float64), axis, -1)
    blocks = v.reshape(v.shape[:-1] + (-1, 32))
    amax = np.abs(blocks).max(-1, keepdims=True)
    byte = np.maximum(np.where(amax > 0, np.frexp(amax)[1] - 1 + 127, 0) - down, 1)
    scale = np.exp2(byte - 127.0)
    codes = (blocks / scale).astype(np.float32).astype(dtype).astype(np.float64)
    return np.moveaxis((codes * scale).reshape(v.shape), -1, axis)


WIDE = False


def mx_kscale(k):
    if not WIDE:
        return np.ones(k)
    levels = np.array([10, -10, 5, -5, 0])
    if k % 512:
        return np.exp2(np.random.permutation(np.resize(levels, k // 32))).repeat(32)
    a = np.empty((k // 512, 16))
    for p in range(k // 512):
        a[p, :8] = np.random.permutation(np.resize(levels, 8))
        for g in range(8):
            far = levels[np.abs(levels - a[p, g]) >= 10]
            a[p, g + 8] = far[np.random.randint(len(far))]
    return np.exp2(a.ravel()).repeat(32)


def f64(x):
    return np.asarray(x).astype(np.float64)


def striped(idx):
    return np.tile(idx.reshape(-1, 16).T, (8, 1)).astype(np.uint16)


def unstriped(offs):
    return offs[:16].T.reshape(-1).astype(np.int64)


E2M1 = np.array([0.0, 0.5, 1.0, 1.5, 2.0, 3.0, 4.0, 6.0, -0.0, -0.5, -1.0, -1.5, -2.0, -3.0, -4.0, -6.0])


def pack_weight(w, fmt):
    k, n = w.shape
    w = f64(np.asarray(w, np.float32).astype(ml_dtypes.bfloat16)).reshape(k // 32, 32, n)
    amax = np.abs(w).max(1)
    if fmt == "e4m3":
        byte = np.frexp(amax)[1] - 1 + 127 - 7
    else:
        mant, ex = np.frexp(amax / 6.0)
        byte = np.where(mant > 0.5, ex, ex - 1) + 127
    byte = np.clip(np.where(amax > 0, byte, 1), 1, 254)
    scaled = (w * np.exp2(127.0 - byte)[:, None, :]).reshape(k, n).astype(np.float32)
    by_word = np.ascontiguousarray(scaled.reshape(k // 512, 128, 4, n).transpose(0, 1, 3, 2))
    if fmt == "e4m3":
        words = by_word.astype(ml_dtypes.float8_e4m3fn).view(np.uint8)
    else:
        c = by_word.astype(ml_dtypes.float4_e2m1fn).view(np.uint8) & 0xF
        words = (c[..., 0::2] | (c[..., 1::2] << 4)).reshape(k // 512, 128, 2 * n)
    return np.ascontiguousarray(words), np.ascontiguousarray(byte.astype(np.uint8).reshape(k // 512, 16, n))


def unpack_weight(words, scales, fmt):
    g, _, n = scales.shape
    words = np.ascontiguousarray(words).reshape(g, 128, n, -1)
    if fmt == "e4m3":
        vals = words.view(ml_dtypes.float8_e4m3fn).astype(np.float64)
    else:
        nib = np.empty((g, 128, n, 4), np.uint8)
        nib[..., 0::2] = words & 0xF
        nib[..., 1::2] = words >> 4
        vals = E2M1[nib]
    vals = vals * np.repeat(np.exp2(scales.astype(np.float64) - 127.0), 8, axis=1)[..., None]
    return vals.transpose(0, 1, 3, 2).reshape(g * 512, n)


def gelu(v):
    return 0.5 * v * (1.0 + np.tanh(np.sqrt(2.0 / np.pi) * (v + 0.044715 * v**3)))


K, KA, KB, T, S, H, T3, S2, P = 1024, 512, 512, 4096, 1024, 1024, 2048, 512, 512


def setup_inputs():
    n = np.random.standard_normal
    s = mx_kscale(K)[:, None]
    u = mx_kscale(H)[:, None]
    tab_words, tab_scales = pack_weight(n((K, T)) * s, "e4m3")
    w1 = (n((KA, H)) / np.sqrt(K) / s[:KA] * u.T).astype(np.float32)
    w4_words, w4_scales = pack_weight(n((KB, H)) / np.sqrt(K) / s[KA:] * u.T, "e2m1")
    tab2_words, tab2_scales = pack_weight(0.75 * n((H, T3)) / np.sqrt(H) / u, "e4m3")
    return {
        "tab_words": tab_words, "tab_scales": tab_scales,
        "offs": striped(np.random.permutation(T)[:S]),
        "w1": w1,
        "w4_words": w4_words, "w4_scales": w4_scales,
        "place": np.random.uniform(0.5, 1.5, S).astype(np.float32),
        "tab2_words": tab2_words, "tab2_scales": tab2_scales,
        "offs2": striped(np.random.permutation(T3)[:S2]),
        "prior": (0.45 * n((S2, S))).astype(np.float32),
        "sens": np.random.uniform(0.6, 3.0, S2).astype(np.float32),
        "thr": n(S2).astype(np.float32),
        "pos1": striped(np.random.permutation(S)[:P]),
        "pos2": striped(np.random.permutation(S)[:P]),
    }


def reference(tab_words, tab_scales, offs, w1, w4_words, w4_scales, place, tab2_words, tab2_scales, offs2,
              prior, sens, thr, pos1, pos2):
    v = unpack_weight(tab_words, tab_scales, "e4m3")[:, unstriped(offs)]
    v2 = unpack_weight(tab2_words, tab2_scales, "e4m3")[:, unstriped(offs2)]
    w4 = unpack_weight(w4_words, w4_scales, "e2m1")
    h = (mxq(f64(w1), 0, "e4m3").T @ v[:KA] + w4.T @ v[KA:]) * f64(place)[None, :]
    e = (v2.T @ mxq(h, 0, "e4m3")) + f64(prior)
    a = 1.0 / (1.0 + np.exp(-(f64(sens)[:, None] * e[:, unstriped(pos1)] + f64(thr)[:, None])))
    c = e[:, unstriped(pos2)]
    return a * c

@@ -1,0 +1,234 @@
+from contextlib import ExitStack
+
+import concourse.mybir as mybir
+from concourse.masks import make_identity
+
+F32 = mybir.dt.float32
+BF16 = mybir.dt.bfloat16
+I32 = mybir.dt.int32
+U32 = mybir.dt.uint32
+U16 = mybir.dt.uint16
+U8 = mybir.dt.uint8
+FP8X4 = mybir.dt.float8_e4m3fn_x4
+FP4X4 = mybir.dt.float4_e2m1fn_x4
+ACT = mybir.ActivationFunctionType
+ALU = mybir.AluOpType
+
+P = 128
+T, S, H, T3, S2, PICKS = 4096, 1024, 1024, 2048, 512, 512
+BANK = 512
+GROUP = 256
+FLOPS = 2 * 1024 * H * S + 2 * H * S2 * S
+
+
+def tile_list_diet_adviser_scores_kernel(
+    tc, tab_words, tab_scales, offs, w1, w4_words, w4_scales, place, tab2_words, tab2_scales, offs2,
+    prior, sens, thr, pos1, pos2, out,
+):
+    nc = tc.nc
+    with ExitStack() as ctx:
+        keep = ctx.enter_context(tc.tile_pool(name="keep", bufs=1))
+        ring = ctx.enter_context(tc.tile_pool(name="ring", bufs=4))
+        ps_h = ctx.enter_context(tc.psum_pool(name="ps_h", bufs=3))
+        ps_t = ctx.enter_context(tc.psum_pool(name="ps_t", bufs=2))
+        ps_e = ctx.enter_context(tc.psum_pool(name="ps_e", bufs=3))
+
+        def held(shape, dtype, name):
+            return keep.tile(shape, dtype, name=name, align_bytes=64)
+
+        offs_t = held([P, S // 16], U16, "offs_t")
+        offs2_t = held([P, S2 // 16], U16, "offs2_t")
+        pos1_t = held([P, PICKS // 16], U16, "pos1_t")
+        pos2_t = held([P, PICKS // 16], U16, "pos2_t")
+        tab_w = [held([P, T], U32, f"tab_w{a}") for a in range(2)]
+        tab_s = held([P, T], U8, "tab_s")
+        tab2_w = [held([P, T3], U32, f"tab2_w{a}") for a in range(2)]
+        tab2_s = held([P, T3], U8, "tab2_s")
+        w1_raw = [held([P, 4, BANK], F32, f"w1_raw{b}") for b in range(2)]
+        w4_w = held([P, 2 * H], U8, "w4_w")
+        w4_s = held([P, H], U8, "w4_s")
+        prior_t = [held([P, 4, BANK], F32, f"prior_t{half}") for half in range(2)]
+        rows = held([P, P], F32, "rows")
+        ident = held([P, P], F32, "ident")
+        cols = held([P, 16], F32, "cols")
+
+        nc.vector.memset(rows[:], 0.0)
+        nc.vector.memset(w4_s[:].bitcast(I32), 0)
+        nc.vector.memset(tab_s[:].bitcast(I32), 0)
+        nc.vector.memset(tab2_s[:].bitcast(I32), 0)
+
+        def load_words(tile, words):
+            nc.sync.dma_start(out=tile[:].bitcast(I32), in_=words.rearrange("p t i -> p (t i)").bitcast(I32))
+
+        def load_w1(b):
+            nc.sync.dma_start(
+                out=w1_raw[b][:], in_=w1[:, b * BANK : (b + 1) * BANK].rearrange("(p i) c -> p i c", i=4)
+            )
+
+        def load_prior(half):
+            nc.sync.dma_start(
+                out=prior_t[half][:],
+                in_=prior[:, half * BANK : (half + 1) * BANK].rearrange("(m p) j -> p m j", p=P),
+            )
+
+        nc.sync.dma_start(offs_t[:], offs)
+        load_w1(0)
+        nc.sync.dma_start(out=rows[0:8, :], in_=place.rearrange("(c p) -> c p", p=P))
+        nc.sync.dma_start(out=rows[8:12, :], in_=sens.rearrange("(c p) -> c p", p=P))
+        nc.sync.dma_start(out=rows[12:16, :], in_=thr.rearrange("(c p) -> c p", p=P))
+        load_words(tab_w[0], tab_words[0])
+        nc.sync.dma_start(out=w4_w[:].bitcast(I32), in_=w4_words[0].bitcast(I32))
+        for q in range(4):
+            nc.sync.dma_start(
+                out=w4_s[32 * q : 32 * q + 4, :].bitcast(I32), in_=w4_scales[0, 4 * q : 4 * q + 4, :].bitcast(I32)
+            )
+        load_words(tab_w[1], tab_words[1])
+        load_w1(1)
+        nc.sync.dma_start(offs2_t[:], offs2)
+        load_words(tab2_w[0], tab2_words[0])
+        load_words(tab2_w[1], tab2_words[1])
+        load_prior(0)
+        nc.sync.dma_start(pos1_t[:], pos1)
+        nc.sync.dma_start(pos2_t[:], pos2)
+        load_prior(1)
+
+        make_identity(nc, ident[:])
+        TAB_ROW = (4, 0)
+        for a in range(2):
+            for q in range(4):
+                first = 32 * q + TAB_ROW[a]
+                nc.gpsimd.dma_start(
+                    out=tab_s[first : first + 4, :].bitcast(I32),
+                    in_=tab_scales[a, 4 * q : 4 * q + 4, :].bitcast(I32),
+                )
+        for q in range(4):
+            nc.gpsimd.dma_start(
+                out=tab2_s[32 * q : 32 * q + 8, :].bitcast(I32),
+                in_=tab2_scales[:, 4 * q : 4 * q + 4, :].bitcast(I32),
+            )
+
+        w1_bf = [held([P, BANK, 4], BF16, f"w1_bf{b}") for b in range(2)]
+        w1_w = [held([P, BANK], U32, f"w1_w{b}") for b in range(2)]
+        w1_s = [held([P, BANK], U8, f"w1_s{b}") for b in range(2)]
+
+        def round_w1(b, copy):
+            copy(
+                out=w1_bf[b][:].rearrange("p (c n) i -> p c i n", n=4),
+                in_=w1_raw[b][:].rearrange("p i (c n) -> p c i n", n=4),
+            )
+
+        def quantize_w1(b):
+            nc.vector.quantize_mx(
+                out=w1_w[b][:].bitcast(FP8X4), scales=w1_s[b][:], in_=w1_bf[b][:].rearrange("p c i -> p (c i)")
+            )
+
+        v_w = [held([P, S], U32, f"v_w{a}") for a in range(2)]
+        v_s = held([P, S], U8, "v_s")
+        v2_w = [held([P, S2], U32, f"v2_w{a}") for a in range(2)]
+        v2_s = held([P, S2], U8, "v2_s")
+
+        round_w1(0, nc.scalar.copy)
+        turned = ps_t.tile([P, 2, 2, P], F32, name="turned")
+        nc.tensor.transpose(turned[:, 0, 0, :], rows[:], ident[:])
+        nc.scalar.copy(out=cols[:], in_=turned[:, 0, 0, 0:16])
+
+        quantize_w1(0)
+        nc.vector.tensor_copy(out=v_w[0][:], in_=tab_w[0][:].indirect(offs_t[:]))
+        nc.vector.tensor_copy(out=v_s[:], in_=tab_s[:].indirect(offs_t[:]))
+        for j0, j1 in ((0, 256), (256, 512), (512, 1024)):
+            nc.vector.tensor_copy(out=v_w[1][:, j0:j1], in_=tab_w[1][:].indirect(offs_t[:, j0 // 16 : j1 // 16]))
+        round_w1(1, nc.vector.tensor_copy)
+        quantize_w1(1)
+
+        h_w = [held([P, S], U32, f"h_w{b}") for b in range(2)]
+        h_s = [held([P, S], U8, f"h_s{b}") for b in range(2)]
+        e = [held([P, S], F32, f"e{m}") for m in range(4)]
+
+        def features(g, b):
+            tiles = []
+            for jt in range(2):
+                c = 2 * g + jt
+                j = slice(c * P, (c + 1) * P)
+                acc = ps_h.tile([P, BANK], F32, name="acc")
+                nc.tensor.matmul_mx(
+                    out=acc[:], lhsT=v_w[0][:, j].bitcast(FP8X4), lhsT_scale=v_s[TAB_ROW[0] :, j],
+                    rhs=w1_w[b][:].bitcast(FP8X4), rhs_scale=w1_s[b][:], start=True, stop=False,
+                )
+                nc.tensor.matmul_mx(
+                    out=acc[:], lhsT=v_w[1][:, j].bitcast(FP8X4), lhsT_scale=v_s[:, j],
+                    rhs=w4_w[:, 2 * b * BANK : 2 * (b + 1) * BANK].bitcast(FP4X4),
+                    rhs_scale=w4_s[:, b * BANK : (b + 1) * BANK], start=False, stop=True,
+                )
+                hT = ring.tile([P, BANK], BF16, name="hT", align_bytes=64)
+                nc.scalar.activation(
+                    out=hT[:].rearrange("j (u p e) -> j u p e", u=2, e=2),
+                    in_=acc[:].rearrange("j (p u e) -> j u p e", u=2, e=2),
+                    func=ACT.Copy, scale=cols[:, c : c + 1],
+                )
+                tiles.append(hT)
+            return tiles
+
+        def turn(tiles):
+            turned = ps_t.tile([P, 2, 2, P], F32, name="turned")
+            for jt in range(2):
+                for u in range(2):
+                    nc.tensor.transpose(
+                        turned[:, jt, u, :], tiles[jt][:].bitcast(F32)[:, u * P : (u + 1) * P], ident[:]
+                    )
+            h_bf = ring.tile([P, 4 * GROUP], BF16, name="h_bf", align_bytes=64)
+            nc.scalar.copy(
+                out=h_bf[:].bitcast(F32).rearrange("p (t j u) -> p t j u", t=2, u=2),
+                in_=turned[:].rearrange("p t u j -> p t j u"),
+            )
+            return h_bf
+
+        def quantize_h(g, b, h_bf):
+            j = slice(g * GROUP, (g + 1) * GROUP)
+            nc.vector.quantize_mx(out=h_w[b][:, j].bitcast(FP8X4), scales=h_s[b][:, j], in_=h_bf[:])
+
+        def scores(j0, j1):
+            for m in range(4):
+                animals = slice(m * P, (m + 1) * P)
+                acc = ps_e.tile([P, BANK], F32, name="score")
+                for b in range(2):
+                    nc.tensor.matmul_mx(
+                        out=acc[:, 0 : j1 - j0], lhsT=v2_w[b][:, animals].bitcast(FP8X4),
+                        lhsT_scale=v2_s[4 * b :, animals],
+                        rhs=h_w[b][:, j0:j1].bitcast(FP8X4), rhs_scale=h_s[b][:, j0:j1],
+                        start=(b == 0), stop=(b == 1),
+                    )
+                half = j0 // BANK
+                nc.vector.tensor_tensor(
+                    out=e[m][:, j0:j1], in0=acc[:, 0 : j1 - j0],
+                    in1=prior_t[half][:, m, j0 - half * BANK : j1 - half * BANK], op=ALU.add,
+                )
+
+        order = [(0, 0), (1, 0), (0, 1), (1, 1), (2, 0), (2, 1), (3, 0), (3, 1)]
+        made = {}
+        turned_tiles = {}
+        for step in range(len(order) + 2):
+            if step < len(order):
+                made[step] = features(*order[step])
+            if 1 <= step <= len(order):
+                turned_tiles[step - 1] = turn(made[step - 1])
+            if step >= 2:
+                quantize_h(*order[step - 2], turned_tiles[step - 2])
+            if step == 4:
+                nc.vector.tensor_copy(out=v2_s[:], in_=tab2_s[:].indirect(offs2_t[:]))
+                for a in range(2):
+                    nc.vector.tensor_copy(out=v2_w[a][:], in_=tab2_w[a][:].indirect(offs2_t[:]))
+            if step == 5:
+                scores(0, 512)
+            if step == 7:
+                scores(512, 768)
+        scores(768, 1024)
+
+        for m in range(4):
+            bent = ring.tile([P, PICKS], F32, name="bent", align_bytes=64)
+            nc.scalar.activation(
+                out=bent[:], in_=e[m][:].indirect(pos1_t[:]), func=ACT.Sigmoid,
+                scale=cols[:, 8 + m : 9 + m], bias=cols[:, 12 + m : 13 + m],
+            )
+            res = ring.tile([P, PICKS], F32, name="res", align_bytes=64)
+            nc.vector.tensor_tensor(out=res[:], in0=e[m][:].indirect(pos2_t[:]), in1=bent[:], op=ALU.mult)
+            nc.sync.dma_start(out=out[m * P : (m + 1) * P, :], in_=res[:])

@@ -52,9 +52,9 @@ def tile_list_diet_adviser_scores_kernel(
         ident = held([P, P], F32, "ident")
         cols = held([P, 16], F32, "cols")
 
+        nc.vector.memset(tab_s[:].bitcast(I32), 0)
         nc.vector.memset(rows[:], 0.0)
         nc.vector.memset(w4_s[:].bitcast(I32), 0)
-        nc.vector.memset(tab_s[:].bitcast(I32), 0)
         nc.vector.memset(tab2_s[:].bitcast(I32), 0)
 
         def load_words(tile, words):
@@ -71,41 +71,45 @@ def tile_list_diet_adviser_scores_kernel(
                 in_=prior[:, half * BANK : (half + 1) * BANK].rearrange("(m p) j -> p m j", p=P),
             )
 
+        TAB_ROW = (4, 0)
+
+        def load_tab_scales(a, q):
+            first = 32 * q + TAB_ROW[a]
+            nc.sync.dma_start(
+                out=tab_s[first : first + 4, :].bitcast(I32), in_=tab_scales[a, 4 * q : 4 * q + 4, :].bitcast(I32)
+            )
+
+        quadrants = [(a, q) for a in range(2) for q in range(4)]
         nc.sync.dma_start(offs_t[:], offs)
         load_w1(0)
+        for a, q in quadrants[:6]:
+            load_tab_scales(a, q)
+        load_words(tab_w[0], tab_words[0])
+        for a, q in quadrants[6:]:
+            load_tab_scales(a, q)
         nc.sync.dma_start(out=rows[0:8, :], in_=place.rearrange("(c p) -> c p", p=P))
         nc.sync.dma_start(out=rows[8:12, :], in_=sens.rearrange("(c p) -> c p", p=P))
         nc.sync.dma_start(out=rows[12:16, :], in_=thr.rearrange("(c p) -> c p", p=P))
-        load_words(tab_w[0], tab_words[0])
         nc.sync.dma_start(out=w4_w[:].bitcast(I32), in_=w4_words[0].bitcast(I32))
+        load_words(tab_w[1], tab_words[1])
         for q in range(4):
             nc.sync.dma_start(
                 out=w4_s[32 * q : 32 * q + 4, :].bitcast(I32), in_=w4_scales[0, 4 * q : 4 * q + 4, :].bitcast(I32)
             )
-        load_words(tab_w[1], tab_words[1])
         load_w1(1)
         nc.sync.dma_start(offs2_t[:], offs2)
         load_words(tab2_w[0], tab2_words[0])
         load_words(tab2_w[1], tab2_words[1])
+        for q in range(4):
+            nc.sync.dma_start(
+                out=tab2_s[32 * q : 32 * q + 8, :].bitcast(I32),
+                in_=tab2_scales[:, 4 * q : 4 * q + 4, :].bitcast(I32),
+            )
         load_prior(0)
         nc.sync.dma_start(pos1_t[:], pos1)
         nc.sync.dma_start(pos2_t[:], pos2)
         load_prior(1)
-
         make_identity(nc, ident[:])
-        TAB_ROW = (4, 0)
-        for a in range(2):
-            for q in range(4):
-                first = 32 * q + TAB_ROW[a]
-                nc.gpsimd.dma_start(
-                    out=tab_s[first : first + 4, :].bitcast(I32),
-                    in_=tab_scales[a, 4 * q : 4 * q + 4, :].bitcast(I32),
-                )
-        for q in range(4):
-            nc.gpsimd.dma_start(
-                out=tab2_s[32 * q : 32 * q + 8, :].bitcast(I32),
-                in_=tab2_scales[:, 4 * q : 4 * q + 4, :].bitcast(I32),
-            )
 
         w1_bf = [held([P, BANK, 4], BF16, f"w1_bf{b}") for b in range(2)]
         w1_w = [held([P, BANK], U32, f"w1_w{b}") for b in range(2)]
@@ -214,9 +218,9 @@ def tile_list_diet_adviser_scores_kernel(
             if step >= 2:
                 quantize_h(*order[step - 2], turned_tiles[step - 2])
             if step == 4:
-                nc.vector.tensor_copy(out=v2_s[:], in_=tab2_s[:].indirect(offs2_t[:]))
                 for a in range(2):
                     nc.vector.tensor_copy(out=v2_w[a][:], in_=tab2_w[a][:].indirect(offs2_t[:]))
+                nc.vector.tensor_copy(out=v2_s[:], in_=tab2_s[:].indirect(offs2_t[:]))
             if step == 5:
                 scores(0, 512)
             if step == 7:

@@ -28,7 +28,7 @@ def tile_list_diet_adviser_scores_kernel(
     nc = tc.nc
     with ExitStack() as ctx:
         keep = ctx.enter_context(tc.tile_pool(name="keep", bufs=1))
-        ring = ctx.enter_context(tc.tile_pool(name="ring", bufs=4))
+        ring = ctx.enter_context(tc.tile_pool(name="ring", bufs=6))
         ps_h = ctx.enter_context(tc.psum_pool(name="ps_h", bufs=3))
         ps_t = ctx.enter_context(tc.psum_pool(name="ps_t", bufs=2))
         ps_e = ctx.enter_context(tc.psum_pool(name="ps_e", bufs=3))
@@ -47,68 +47,63 @@ def tile_list_diet_adviser_scores_kernel(
         w1_raw = [held([P, 4, BANK], F32, f"w1_raw{b}") for b in range(2)]
         w4_w = held([P, 2 * H], U8, "w4_w")
         w4_s = held([P, H], U8, "w4_s")
-        prior_t = [held([P, 4, BANK], F32, f"prior_t{half}") for half in range(2)]
+        prior_low = held([P, 4, BANK], F32, "prior_low")
+        prior_high = [held([P, BANK], F32, f"prior_high{m}") for m in range(4)]
         rows = held([P, P], F32, "rows")
         ident = held([P, P], F32, "ident")
         cols = held([P, 16], F32, "cols")
 
+        nc.gpsimd.memset(rows[:], 0.0)
         nc.vector.memset(tab_s[:].bitcast(I32), 0)
-        nc.vector.memset(rows[:], 0.0)
         nc.vector.memset(w4_s[:].bitcast(I32), 0)
         nc.vector.memset(tab2_s[:].bitcast(I32), 0)
 
         def load_words(tile, words):
-            nc.sync.dma_start(out=tile[:].bitcast(I32), in_=words.rearrange("p t i -> p (t i)").bitcast(I32))
+            nc.sync.dma_start(out=tile.bitcast(I32), in_=words.rearrange("p t i -> p (t i)").bitcast(I32))
 
         def load_w1(b):
             nc.sync.dma_start(
                 out=w1_raw[b][:], in_=w1[:, b * BANK : (b + 1) * BANK].rearrange("(p i) c -> p i c", i=4)
             )
 
-        def load_prior(half):
-            nc.sync.dma_start(
-                out=prior_t[half][:],
-                in_=prior[:, half * BANK : (half + 1) * BANK].rearrange("(m p) j -> p m j", p=P),
-            )
-
         TAB_ROW = (4, 0)
 
-        def load_tab_scales(a, q):
-            first = 32 * q + TAB_ROW[a]
+        def load_tab_scales(a, r):
             nc.sync.dma_start(
-                out=tab_s[first : first + 4, :].bitcast(I32), in_=tab_scales[a, 4 * q : 4 * q + 4, :].bitcast(I32)
+                out=tab_s[TAB_ROW[a] + r : P : 32, :].bitcast(I32), in_=tab_scales[a, r:16:4, :].bitcast(I32)
             )
 
-        quadrants = [(a, q) for a in range(2) for q in range(4)]
+        quadrants = [(a, r) for r in range(4) for a in range(2)]
         nc.sync.dma_start(offs_t[:], offs)
         load_w1(0)
-        for a, q in quadrants[:6]:
-            load_tab_scales(a, q)
-        load_words(tab_w[0], tab_words[0])
-        for a, q in quadrants[6:]:
-            load_tab_scales(a, q)
         nc.sync.dma_start(out=rows[0:8, :], in_=place.rearrange("(c p) -> c p", p=P))
         nc.sync.dma_start(out=rows[8:12, :], in_=sens.rearrange("(c p) -> c p", p=P))
         nc.sync.dma_start(out=rows[12:16, :], in_=thr.rearrange("(c p) -> c p", p=P))
+        for a, q in quadrants[:3]:
+            load_tab_scales(a, q)
+        load_words(tab_w[0][:, 0 : T // 2], tab_words[0, :, 0 : T // 2, :])
+        for a, q in quadrants[3:]:
+            load_tab_scales(a, q)
+        load_words(tab_w[0][:, T // 2 : T], tab_words[0, :, T // 2 : T, :])
         nc.sync.dma_start(out=w4_w[:].bitcast(I32), in_=w4_words[0].bitcast(I32))
-        load_words(tab_w[1], tab_words[1])
-        for q in range(4):
-            nc.sync.dma_start(
-                out=w4_s[32 * q : 32 * q + 4, :].bitcast(I32), in_=w4_scales[0, 4 * q : 4 * q + 4, :].bitcast(I32)
-            )
+        load_words(tab_w[1][:, 0 : T // 2], tab_words[1, :, 0 : T // 2, :])
+        for r in range(4):
+            nc.sync.dma_start(out=w4_s[r:P:32, :].bitcast(I32), in_=w4_scales[0, r:16:4, :].bitcast(I32))
+        load_words(tab_w[1][:, T // 2 : T], tab_words[1, :, T // 2 : T, :])
         load_w1(1)
         nc.sync.dma_start(offs2_t[:], offs2)
-        load_words(tab2_w[0], tab2_words[0])
-        load_words(tab2_w[1], tab2_words[1])
+        load_words(tab2_w[0][:], tab2_words[0])
+        load_words(tab2_w[1][:], tab2_words[1])
         for q in range(4):
             nc.sync.dma_start(
-                out=tab2_s[32 * q : 32 * q + 8, :].bitcast(I32),
+                out=tab2_s[32 * q + 8 : 32 * q + 16, :].bitcast(I32),
                 in_=tab2_scales[:, 4 * q : 4 * q + 4, :].bitcast(I32),
             )
-        load_prior(0)
+        nc.sync.dma_start(out=prior_low[:], in_=prior[:, 0:BANK].rearrange("(m p) j -> p m j", p=P))
         nc.sync.dma_start(pos1_t[:], pos1)
         nc.sync.dma_start(pos2_t[:], pos2)
-        load_prior(1)
+        for m in range(4):
+            nc.sync.dma_start(out=prior_high[m][:], in_=prior[m * P : (m + 1) * P, BANK:S])
         make_identity(nc, ident[:])
 
         w1_bf = [held([P, BANK, 4], BF16, f"w1_bf{b}") for b in range(2)]
@@ -131,101 +126,170 @@ def tile_list_diet_adviser_scores_kernel(
         v2_w = [held([P, S2], U32, f"v2_w{a}") for a in range(2)]
         v2_s = held([P, S2], U8, "v2_s")
 
-        round_w1(0, nc.scalar.copy)
+        nc.scalar.copy(
+            out=w1_bf[0][:].rearrange("p (t m) i -> p m i t", t=4),
+            in_=w1_raw[0][:].rearrange("p i (m t) -> p m i t", t=4),
+        )
         turned = ps_t.tile([P, 2, 2, P], F32, name="turned")
         nc.tensor.transpose(turned[:, 0, 0, :], rows[:], ident[:])
         nc.scalar.copy(out=cols[:], in_=turned[:, 0, 0, 0:16])
+        place_all = held([P, S], F32, "place_all")
+        for half in range(2):
+            turned = ps_t.tile([P, 2, 2, P], F32, name="turned")
+            for n in range(4):
+                c = 4 * half + n
+                if c >= 2:
+                    nc.tensor.transpose(
+                        turned[:, n // 2, n % 2, :], cols[:, c : c + 1].to_broadcast([P, P]), ident[:]
+                    )
+            first = max(2 - 4 * half, 0) * P
+            if first < BANK:
+                nc.scalar.copy(
+                    out=place_all[:, half * BANK + first : (half + 1) * BANK],
+                    in_=turned[:].rearrange("p a b j -> p (a b j)")[:, first:BANK],
+                )
 
         quantize_w1(0)
-        nc.vector.tensor_copy(out=v_w[0][:], in_=tab_w[0][:].indirect(offs_t[:]))
         nc.vector.tensor_copy(out=v_s[:], in_=tab_s[:].indirect(offs_t[:]))
-        for j0, j1 in ((0, 256), (256, 512), (512, 1024)):
+        nc.vector.tensor_copy(out=v_w[0][:], in_=tab_w[0][:].indirect(offs_t[:]))
+        w4d_w = held([P, 2 * BANK], U8, "w4d_w")
+        w4d_s = held([P, BANK], U8, "w4d_s")
+        nc.vector.tensor_copy(
+            out=w4d_w[:].rearrange("p (t m y) -> p t m y", t=4, y=2),
+            in_=w4_w[:, 0 : 2 * BANK].rearrange("p (m t y) -> p t m y", t=4, y=2),
+        )
+        nc.vector.tensor_copy(
+            out=w4d_s[:].rearrange("p (t m) -> p t m", t=4),
+            in_=w4_s[:, 0:BANK].rearrange("p (m t) -> p t m", t=4),
+        )
+        w4_words_of = (w4d_w[:], w4_w[:, 2 * BANK : 4 * BANK])
+        w4_scales_of = (w4d_s[:], w4_s[:, BANK : 2 * BANK])
+        PAIRS_OF = ("j (u e p) -> j u p e", "j (p u e) -> j u p e")
+
+        def gather_tab1(j0, j1):
             nc.vector.tensor_copy(out=v_w[1][:, j0:j1], in_=tab_w[1][:].indirect(offs_t[:, j0 // 16 : j1 // 16]))
-        round_w1(1, nc.vector.tensor_copy)
-        quantize_w1(1)
 
         h_w = [held([P, S], U32, f"h_w{b}") for b in range(2)]
         h_s = [held([P, S], U8, f"h_s{b}") for b in range(2)]
         e = [held([P, S], F32, f"e{m}") for m in range(4)]
 
-        def features(g, b):
+        def features(units):
+            hT = ring.tile([P, 4, BANK], BF16, name="hT", align_bytes=64)
+            for n, (g, b) in enumerate(units):
+                for jt in range(2):
+                    c = 2 * g + jt
+                    j = slice(c * P, (c + 1) * P)
+                    acc = ps_h.tile([P, BANK], F32, name="acc")
+                    nc.tensor.matmul_mx(
+                        out=acc[:], lhsT=v_w[0][:, j].bitcast(FP8X4), lhsT_scale=v_s[TAB_ROW[0] :, j],
+                        rhs=w1_w[b][:].bitcast(FP8X4), rhs_scale=w1_s[b][:], start=True, stop=False,
+                    )
+                    nc.tensor.matmul_mx(
+                        out=acc[:], lhsT=v_w[1][:, j].bitcast(FP8X4), lhsT_scale=v_s[:, j],
+                        rhs=w4_words_of[b].bitcast(FP4X4), rhs_scale=w4_scales_of[b], start=False, stop=True,
+                    )
+                    nc.scalar.activation(
+                        out=hT[:, 2 * n + jt, :].rearrange("j (u p e) -> j u p e", u=2, e=2),
+                        in_=acc[:].rearrange(PAIRS_OF[b], u=2, e=2),
+                        func=ACT.Copy, scale=cols[:, c : c + 1],
+                    )
+            return hT
+
+        def turn(units, hT, copies):
+            words = hT[:].bitcast(F32)
+            banks = []
+            for n in range(len(units)):
+                turned = ps_t.tile([P, 2, 2, P], F32, name="turned")
+                for jt in range(2):
+                    for u in range(2):
+                        nc.tensor.transpose(
+                            turned[:, jt, u, :], words[:, 2 * n + jt, u * P : (u + 1) * P], ident[:]
+                        )
+                banks.append(turned)
             tiles = []
+            for turned, copy in zip(banks, copies):
+                h_bf = ring.tile([P, 4 * GROUP], BF16, name="h_bf", align_bytes=64)
+                copy(
+                    out=h_bf[:].bitcast(F32).rearrange("p (t j u) -> p t j u", t=2, u=2),
+                    in_=turned[:].rearrange("p t u j -> p t j u"),
+                )
+                tiles.append(h_bf)
+            return tiles
+
+        def direct(g):
+            h_bf = ring.tile([P, 4 * GROUP], BF16, name="h_bf", align_bytes=64)
             for jt in range(2):
                 c = 2 * g + jt
                 j = slice(c * P, (c + 1) * P)
-                acc = ps_h.tile([P, BANK], F32, name="acc")
-                nc.tensor.matmul_mx(
-                    out=acc[:], lhsT=v_w[0][:, j].bitcast(FP8X4), lhsT_scale=v_s[TAB_ROW[0] :, j],
-                    rhs=w1_w[b][:].bitcast(FP8X4), rhs_scale=w1_s[b][:], start=True, stop=False,
-                )
-                nc.tensor.matmul_mx(
-                    out=acc[:], lhsT=v_w[1][:, j].bitcast(FP8X4), lhsT_scale=v_s[:, j],
-                    rhs=w4_w[:, 2 * b * BANK : 2 * (b + 1) * BANK].bitcast(FP4X4),
-                    rhs_scale=w4_s[:, b * BANK : (b + 1) * BANK], start=False, stop=True,
-                )
-                hT = ring.tile([P, BANK], BF16, name="hT", align_bytes=64)
-                nc.scalar.activation(
-                    out=hT[:].rearrange("j (u p e) -> j u p e", u=2, e=2),
-                    in_=acc[:].rearrange("j (p u e) -> j u p e", u=2, e=2),
-                    func=ACT.Copy, scale=cols[:, c : c + 1],
-                )
-                tiles.append(hT)
-            return tiles
-
-        def turn(tiles):
-            turned = ps_t.tile([P, 2, 2, P], F32, name="turned")
-            for jt in range(2):
-                for u in range(2):
-                    nc.tensor.transpose(
-                        turned[:, jt, u, :], tiles[jt][:].bitcast(F32)[:, u * P : (u + 1) * P], ident[:]
+                acc = ps_e.tile([P, BANK], F32, name="score")
+                for t in range(4):
+                    r = slice(t * P, (t + 1) * P)
+                    nc.tensor.matmul_mx(
+                        out=acc[:, r], lhsT=w1_w[0][:, r].bitcast(FP8X4), lhsT_scale=w1_s[0][:, r],
+                        rhs=v_w[0][:, j].bitcast(FP8X4), rhs_scale=v_s[TAB_ROW[0] :, j], start=(t == 0), stop=False,
                     )
-            h_bf = ring.tile([P, 4 * GROUP], BF16, name="h_bf", align_bytes=64)
-            nc.scalar.copy(
-                out=h_bf[:].bitcast(F32).rearrange("p (t j u) -> p t j u", t=2, u=2),
-                in_=turned[:].rearrange("p t u j -> p t j u"),
-            )
+                for t in range(4):
+                    r = slice(t * P, (t + 1) * P)
+                    nc.tensor.matmul_mx(
+                        out=acc[:, r], lhsT=w4d_w[:, 2 * t * P : 2 * (t + 1) * P].bitcast(FP4X4),
+                        lhsT_scale=w4d_s[:, r],
+                        rhs=v_w[1][:, j].bitcast(FP8X4), rhs_scale=v_s[:, j], start=False, stop=(t == 3),
+                    )
+                nc.vector.tensor_tensor(
+                    out=h_bf[:, jt * BANK : (jt + 1) * BANK].rearrange("p (j t) -> p j t", t=4),
+                    in0=acc[:].rearrange("p (t j) -> p j t", t=4),
+                    in1=place_all[:, j].unsqueeze(2).to_broadcast([P, P, 4]),
+                    op=ALU.mult,
+                )
             return h_bf
 
         def quantize_h(g, b, h_bf):
             j = slice(g * GROUP, (g + 1) * GROUP)
             nc.vector.quantize_mx(out=h_w[b][:, j].bitcast(FP8X4), scales=h_s[b][:, j], in_=h_bf[:])
 
-        def scores(j0, j1):
-            for m in range(4):
-                animals = slice(m * P, (m + 1) * P)
-                acc = ps_e.tile([P, BANK], F32, name="score")
-                for b in range(2):
-                    nc.tensor.matmul_mx(
-                        out=acc[:, 0 : j1 - j0], lhsT=v2_w[b][:, animals].bitcast(FP8X4),
-                        lhsT_scale=v2_s[4 * b :, animals],
-                        rhs=h_w[b][:, j0:j1].bitcast(FP8X4), rhs_scale=h_s[b][:, j0:j1],
-                        start=(b == 0), stop=(b == 1),
-                    )
-                half = j0 // BANK
-                nc.vector.tensor_tensor(
-                    out=e[m][:, j0:j1], in0=acc[:, 0 : j1 - j0],
-                    in1=prior_t[half][:, m, j0 - half * BANK : j1 - half * BANK], op=ALU.add,
+        def scores(m, half, prior_part):
+            animals = slice(m * P, (m + 1) * P)
+            j = slice(half * BANK, (half + 1) * BANK)
+            acc = ps_e.tile([P, BANK], F32, name="score")
+            for b in range(2):
+                nc.tensor.matmul_mx(
+                    out=acc[:], lhsT=v2_w[b][:, animals].bitcast(FP8X4), lhsT_scale=v2_s[8 + 4 * b :, animals],
+                    rhs=h_w[b][:, j].bitcast(FP8X4), rhs_scale=h_s[b][:, j], start=(b == 0), stop=(b == 1),
                 )
+            nc.vector.tensor_tensor(out=e[m][:, j], in0=acc[:], in1=prior_part, op=ALU.add)
 
-        order = [(0, 0), (1, 0), (0, 1), (1, 1), (2, 0), (2, 1), (3, 0), (3, 1)]
-        made = {}
-        turned_tiles = {}
-        for step in range(len(order) + 2):
-            if step < len(order):
-                made[step] = features(*order[step])
-            if 1 <= step <= len(order):
-                turned_tiles[step - 1] = turn(made[step - 1])
-            if step >= 2:
-                quantize_h(*order[step - 2], turned_tiles[step - 2])
-            if step == 4:
-                for a in range(2):
-                    nc.vector.tensor_copy(out=v2_w[a][:], in_=tab2_w[a][:].indirect(offs2_t[:]))
-                nc.vector.tensor_copy(out=v2_s[:], in_=tab2_s[:].indirect(offs2_t[:]))
-            if step == 5:
-                scores(0, 512)
-            if step == 7:
-                scores(512, 768)
-        scores(768, 1024)
+        sc = nc.scalar.copy
+
+        def turned_units(units, hT):
+            for (g, b), h_bf in zip(units, turn(units, hT, [sc] * len(units))):
+                quantize_h(g, b, h_bf)
+
+        gather_tab1(0, 256)
+        gather_tab1(256, 512)
+        first_unit = features([(0, 0)])
+        gather_tab1(512, 1024)
+        round_w1(1, nc.scalar.copy)
+        quantize_w1(1)
+        d1 = direct(1)
+        turned_units([(0, 0)], first_unit)
+        d2 = direct(2)
+        quantize_h(1, 0, d1)
+        low = features([(0, 1), (1, 1)])
+        d3 = direct(3)
+        quantize_h(2, 0, d2)
+        turned_units([(0, 1), (1, 1)], low)
+        third = features([(2, 1)])
+        nc.vector.tensor_copy(out=v2_w[0][:], in_=tab2_w[0][:].indirect(offs2_t[:]))
+        quantize_h(3, 0, d3)
+        nc.vector.tensor_copy(out=v2_w[1][:], in_=tab2_w[1][:].indirect(offs2_t[:]))
+        nc.vector.tensor_copy(out=v2_s[:], in_=tab2_s[:].indirect(offs2_t[:]))
+        last = features([(3, 1)])
+        turned_units([(2, 1)], third)
+        turned_units([(3, 1)], last)
+        for m in range(4):
+            scores(m, 0, prior_low[:, m, :])
+        for m in range(4):
+            scores(m, 1, prior_high[m][:])
 
         for m in range(4):
             bent = ring.tile([P, PICKS], F32, name="bent", align_bytes=64)

from contextlib import ExitStack

import concourse.mybir as mybir
from concourse.masks import make_identity

F32 = mybir.dt.float32
BF16 = mybir.dt.bfloat16
I32 = mybir.dt.int32
U32 = mybir.dt.uint32
U16 = mybir.dt.uint16
U8 = mybir.dt.uint8
FP8X4 = mybir.dt.float8_e4m3fn_x4
FP4X4 = mybir.dt.float4_e2m1fn_x4
ACT = mybir.ActivationFunctionType
ALU = mybir.AluOpType

P = 128
T, S, H, T3, S2, PICKS = 4096, 1024, 1024, 2048, 512, 512
BANK = 512
GROUP = 256
FLOPS = 2 * 1024 * H * S + 2 * H * S2 * S


def tile_list_diet_adviser_scores_kernel(
    tc, tab_words, tab_scales, offs, w1, w4_words, w4_scales, place, tab2_words, tab2_scales, offs2,
    prior, sens, thr, pos1, pos2, out,
):
    nc = tc.nc
    with ExitStack() as ctx:
        keep = ctx.enter_context(tc.tile_pool(name="keep", bufs=1))
        ring = ctx.enter_context(tc.tile_pool(name="ring", bufs=6))
        ps_h = ctx.enter_context(tc.psum_pool(name="ps_h", bufs=3))
        ps_t = ctx.enter_context(tc.psum_pool(name="ps_t", bufs=2))
        ps_e = ctx.enter_context(tc.psum_pool(name="ps_e", bufs=3))

        def held(shape, dtype, name):
            return keep.tile(shape, dtype, name=name, align_bytes=64)

        offs_t = held([P, S // 16], U16, "offs_t")
        offs2_t = held([P, S2 // 16], U16, "offs2_t")
        pos1_t = held([P, PICKS // 16], U16, "pos1_t")
        pos2_t = held([P, PICKS // 16], U16, "pos2_t")
        tab_w = [held([P, T], U32, f"tab_w{a}") for a in range(2)]
        tab_s = held([P, T], U8, "tab_s")
        tab2_w = [held([P, T3], U32, f"tab2_w{a}") for a in range(2)]
        tab2_s = held([P, T3], U8, "tab2_s")
        w1_raw = [held([P, 4, BANK], F32, f"w1_raw{b}") for b in range(2)]
        w4_w = held([P, 2 * H], U8, "w4_w")
        w4_s = held([P, H], U8, "w4_s")
        prior_low = held([P, 4, BANK], F32, "prior_low")
        prior_high = [held([P, BANK], F32, f"prior_high{m}") for m in range(4)]
        rows = held([P, P], F32, "rows")
        ident = held([P, P], F32, "ident")
        cols = held([P, 16], F32, "cols")

        nc.gpsimd.memset(rows[:], 0.0)
        nc.vector.memset(tab_s[:].bitcast(I32), 0)
        nc.vector.memset(w4_s[:].bitcast(I32), 0)
        nc.vector.memset(tab2_s[:].bitcast(I32), 0)

        def load_words(tile, words):
            nc.sync.dma_start(out=tile.bitcast(I32), in_=words.rearrange("p t i -> p (t i)").bitcast(I32))

        def load_w1(b):
            nc.sync.dma_start(
                out=w1_raw[b][:], in_=w1[:, b * BANK : (b + 1) * BANK].rearrange("(p i) c -> p i c", i=4)
            )

        TAB_ROW = (4, 0)

        def load_tab_scales(a, r):
            nc.sync.dma_start(
                out=tab_s[TAB_ROW[a] + r : P : 32, :].bitcast(I32), in_=tab_scales[a, r:16:4, :].bitcast(I32)
            )

        quadrants = [(a, r) for r in range(4) for a in range(2)]
        nc.sync.dma_start(offs_t[:], offs)
        load_w1(0)
        nc.sync.dma_start(out=rows[0:8, :], in_=place.rearrange("(c p) -> c p", p=P))
        nc.sync.dma_start(out=rows[8:12, :], in_=sens.rearrange("(c p) -> c p", p=P))
        nc.sync.dma_start(out=rows[12:16, :], in_=thr.rearrange("(c p) -> c p", p=P))
        for a, q in quadrants[:3]:
            load_tab_scales(a, q)
        load_words(tab_w[0][:, 0 : T // 2], tab_words[0, :, 0 : T // 2, :])
        for a, q in quadrants[3:]:
            load_tab_scales(a, q)
        load_words(tab_w[0][:, T // 2 : T], tab_words[0, :, T // 2 : T, :])
        nc.sync.dma_start(out=w4_w[:].bitcast(I32), in_=w4_words[0].bitcast(I32))
        load_words(tab_w[1][:, 0 : T // 2], tab_words[1, :, 0 : T // 2, :])
        for r in range(4):
            nc.sync.dma_start(out=w4_s[r:P:32, :].bitcast(I32), in_=w4_scales[0, r:16:4, :].bitcast(I32))
        load_words(tab_w[1][:, T // 2 : T], tab_words[1, :, T // 2 : T, :])
        load_w1(1)
        nc.sync.dma_start(offs2_t[:], offs2)
        load_words(tab2_w[0][:], tab2_words[0])
        load_words(tab2_w[1][:], tab2_words[1])
        for q in range(4):
            nc.sync.dma_start(
                out=tab2_s[32 * q + 8 : 32 * q + 16, :].bitcast(I32),
                in_=tab2_scales[:, 4 * q : 4 * q + 4, :].bitcast(I32),
            )
        nc.sync.dma_start(out=prior_low[:], in_=prior[:, 0:BANK].rearrange("(m p) j -> p m j", p=P))
        nc.sync.dma_start(pos1_t[:], pos1)
        nc.sync.dma_start(pos2_t[:], pos2)
        for m in range(4):
            nc.sync.dma_start(out=prior_high[m][:], in_=prior[m * P : (m + 1) * P, BANK:S])
        make_identity(nc, ident[:])

        w1_bf = [held([P, BANK, 4], BF16, f"w1_bf{b}") for b in range(2)]
        w1_w = [held([P, BANK], U32, f"w1_w{b}") for b in range(2)]
        w1_s = [held([P, BANK], U8, f"w1_s{b}") for b in range(2)]

        def round_w1(b, copy):
            copy(
                out=w1_bf[b][:].rearrange("p (c n) i -> p c i n", n=4),
                in_=w1_raw[b][:].rearrange("p i (c n) -> p c i n", n=4),
            )

        def quantize_w1(b):
            nc.vector.quantize_mx(
                out=w1_w[b][:].bitcast(FP8X4), scales=w1_s[b][:], in_=w1_bf[b][:].rearrange("p c i -> p (c i)")
            )

        v_w = [held([P, S], U32, f"v_w{a}") for a in range(2)]
        v_s = held([P, S], U8, "v_s")
        v2_w = [held([P, S2], U32, f"v2_w{a}") for a in range(2)]
        v2_s = held([P, S2], U8, "v2_s")

        nc.scalar.copy(
            out=w1_bf[0][:].rearrange("p (t m) i -> p m i t", t=4),
            in_=w1_raw[0][:].rearrange("p i (m t) -> p m i t", t=4),
        )
        turned = ps_t.tile([P, 2, 2, P], F32, name="turned")
        nc.tensor.transpose(turned[:, 0, 0, :], rows[:], ident[:])
        nc.scalar.copy(out=cols[:], in_=turned[:, 0, 0, 0:16])
        place_all = held([P, S], F32, "place_all")
        for half in range(2):
            turned = ps_t.tile([P, 2, 2, P], F32, name="turned")
            for n in range(4):
                c = 4 * half + n
                if c >= 2:
                    nc.tensor.transpose(
                        turned[:, n // 2, n % 2, :], cols[:, c : c + 1].to_broadcast([P, P]), ident[:]
                    )
            first = max(2 - 4 * half, 0) * P
            if first < BANK:
                nc.scalar.copy(
                    out=place_all[:, half * BANK + first : (half + 1) * BANK],
                    in_=turned[:].rearrange("p a b j -> p (a b j)")[:, first:BANK],
                )

        quantize_w1(0)
        nc.vector.tensor_copy(out=v_s[:], in_=tab_s[:].indirect(offs_t[:]))
        nc.vector.tensor_copy(out=v_w[0][:], in_=tab_w[0][:].indirect(offs_t[:]))
        w4d_w = held([P, 2 * BANK], U8, "w4d_w")
        w4d_s = held([P, BANK], U8, "w4d_s")
        nc.vector.tensor_copy(
            out=w4d_w[:].rearrange("p (t m y) -> p t m y", t=4, y=2),
            in_=w4_w[:, 0 : 2 * BANK].rearrange("p (m t y) -> p t m y", t=4, y=2),
        )
        nc.vector.tensor_copy(
            out=w4d_s[:].rearrange("p (t m) -> p t m", t=4),
            in_=w4_s[:, 0:BANK].rearrange("p (m t) -> p t m", t=4),
        )
        w4_words_of = (w4d_w[:], w4_w[:, 2 * BANK : 4 * BANK])
        w4_scales_of = (w4d_s[:], w4_s[:, BANK : 2 * BANK])
        PAIRS_OF = ("j (u e p) -> j u p e", "j (p u e) -> j u p e")

        def gather_tab1(j0, j1):
            nc.vector.tensor_copy(out=v_w[1][:, j0:j1], in_=tab_w[1][:].indirect(offs_t[:, j0 // 16 : j1 // 16]))

        h_w = [held([P, S], U32, f"h_w{b}") for b in range(2)]
        h_s = [held([P, S], U8, f"h_s{b}") for b in range(2)]
        e = [held([P, S], F32, f"e{m}") for m in range(4)]

        def features(units):
            hT = ring.tile([P, 4, BANK], BF16, name="hT", align_bytes=64)
            for n, (g, b) in enumerate(units):
                for jt in range(2):
                    c = 2 * g + jt
                    j = slice(c * P, (c + 1) * P)
                    acc = ps_h.tile([P, BANK], F32, name="acc")
                    nc.tensor.matmul_mx(
                        out=acc[:], lhsT=v_w[0][:, j].bitcast(FP8X4), lhsT_scale=v_s[TAB_ROW[0] :, j],
                        rhs=w1_w[b][:].bitcast(FP8X4), rhs_scale=w1_s[b][:], start=True, stop=False,
                    )
                    nc.tensor.matmul_mx(
                        out=acc[:], lhsT=v_w[1][:, j].bitcast(FP8X4), lhsT_scale=v_s[:, j],
                        rhs=w4_words_of[b].bitcast(FP4X4), rhs_scale=w4_scales_of[b], start=False, stop=True,
                    )
                    nc.scalar.activation(
                        out=hT[:, 2 * n + jt, :].rearrange("j (u p e) -> j u p e", u=2, e=2),
                        in_=acc[:].rearrange(PAIRS_OF[b], u=2, e=2),
                        func=ACT.Copy, scale=cols[:, c : c + 1],
                    )
            return hT

        def turn(units, hT, copies):
            words = hT[:].bitcast(F32)
            banks = []
            for n in range(len(units)):
                turned = ps_t.tile([P, 2, 2, P], F32, name="turned")
                for jt in range(2):
                    for u in range(2):
                        nc.tensor.transpose(
                            turned[:, jt, u, :], words[:, 2 * n + jt, u * P : (u + 1) * P], ident[:]
                        )
                banks.append(turned)
            tiles = []
            for turned, copy in zip(banks, copies):
                h_bf = ring.tile([P, 4 * GROUP], BF16, name="h_bf", align_bytes=64)
                copy(
                    out=h_bf[:].bitcast(F32).rearrange("p (t j u) -> p t j u", t=2, u=2),
                    in_=turned[:].rearrange("p t u j -> p t j u"),
                )
                tiles.append(h_bf)
            return tiles

        def direct(g):
            h_bf = ring.tile([P, 4 * GROUP], BF16, name="h_bf", align_bytes=64)
            for jt in range(2):
                c = 2 * g + jt
                j = slice(c * P, (c + 1) * P)
                acc = ps_e.tile([P, BANK], F32, name="score")
                for t in range(4):
                    r = slice(t * P, (t + 1) * P)
                    nc.tensor.matmul_mx(
                        out=acc[:, r], lhsT=w1_w[0][:, r].bitcast(FP8X4), lhsT_scale=w1_s[0][:, r],
                        rhs=v_w[0][:, j].bitcast(FP8X4), rhs_scale=v_s[TAB_ROW[0] :, j], start=(t == 0), stop=False,
                    )
                for t in range(4):
                    r = slice(t * P, (t + 1) * P)
                    nc.tensor.matmul_mx(
                        out=acc[:, r], lhsT=w4d_w[:, 2 * t * P : 2 * (t + 1) * P].bitcast(FP4X4),
                        lhsT_scale=w4d_s[:, r],
                        rhs=v_w[1][:, j].bitcast(FP8X4), rhs_scale=v_s[:, j], start=False, stop=(t == 3),
                    )
                nc.vector.tensor_tensor(
                    out=h_bf[:, jt * BANK : (jt + 1) * BANK].rearrange("p (j t) -> p j t", t=4),
                    in0=acc[:].rearrange("p (t j) -> p j t", t=4),
                    in1=place_all[:, j].unsqueeze(2).to_broadcast([P, P, 4]),
                    op=ALU.mult,
                )
            return h_bf

        def quantize_h(g, b, h_bf):
            j = slice(g * GROUP, (g + 1) * GROUP)
            nc.vector.quantize_mx(out=h_w[b][:, j].bitcast(FP8X4), scales=h_s[b][:, j], in_=h_bf[:])

        def scores(m, half, prior_part):
            animals = slice(m * P, (m + 1) * P)
            j = slice(half * BANK, (half + 1) * BANK)
            acc = ps_e.tile([P, BANK], F32, name="score")
            for b in range(2):
                nc.tensor.matmul_mx(
                    out=acc[:], lhsT=v2_w[b][:, animals].bitcast(FP8X4), lhsT_scale=v2_s[8 + 4 * b :, animals],
                    rhs=h_w[b][:, j].bitcast(FP8X4), rhs_scale=h_s[b][:, j], start=(b == 0), stop=(b == 1),
                )
            nc.vector.tensor_tensor(out=e[m][:, j], in0=acc[:], in1=prior_part, op=ALU.add)

        sc = nc.scalar.copy

        def turned_units(units, hT):
            for (g, b), h_bf in zip(units, turn(units, hT, [sc] * len(units))):
                quantize_h(g, b, h_bf)

        gather_tab1(0, 256)
        gather_tab1(256, 512)
        first_unit = features([(0, 0)])
        gather_tab1(512, 1024)
        round_w1(1, nc.scalar.copy)
        quantize_w1(1)
        d1 = direct(1)
        turned_units([(0, 0)], first_unit)
        d2 = direct(2)
        quantize_h(1, 0, d1)
        low = features([(0, 1), (1, 1)])
        d3 = direct(3)
        quantize_h(2, 0, d2)
        turned_units([(0, 1), (1, 1)], low)
        third = features([(2, 1)])
        nc.vector.tensor_copy(out=v2_w[0][:], in_=tab2_w[0][:].indirect(offs2_t[:]))
        quantize_h(3, 0, d3)
        nc.vector.tensor_copy(out=v2_w[1][:], in_=tab2_w[1][:].indirect(offs2_t[:]))
        nc.vector.tensor_copy(out=v2_s[:], in_=tab2_s[:].indirect(offs2_t[:]))
        last = features([(3, 1)])
        turned_units([(2, 1)], third)
        turned_units([(3, 1)], last)
        for m in range(4):
            scores(m, 0, prior_low[:, m, :])
        for m in range(4):
            scores(m, 1, prior_high[m][:])

        for m in range(4):
            bent = ring.tile([P, PICKS], F32, name="bent", align_bytes=64)
            nc.scalar.activation(
                out=bent[:], in_=e[m][:].indirect(pos1_t[:]), func=ACT.Sigmoid,
                scale=cols[:, 8 + m : 9 + m], bias=cols[:, 12 + m : 13 + m],
            )
            res = ring.tile([P, PICKS], F32, name="res", align_bytes=64)
            nc.vector.tensor_tensor(out=res[:], in0=e[m][:].indirect(pos2_t[:]), in1=bent[:], op=ALU.mult)
            nc.sync.dma_start(out=out[m * P : (m + 1) * P, :], in_=res[:])
